import numpy as np
import ml_dtypes


def mxq(x, axis, fmt="e4m3"):
    dtype, down = {"e4m3": (ml_dtypes.float8_e4m3fn, 7), "e5m2": (ml_dtypes.float8_e5m2, 14)}[fmt]
    v = np.moveaxis(np.asarray(x, np.float32).astype(ml_dtypes.bfloat16).astype(np.float64), axis, -1)
    blocks = v.reshape(v.shape[:-1] + (-1, 32))
    amax = np.abs(blocks).max(-1, keepdims=True)
    byte = np.maximum(np.where(amax > 0, np.frexp(amax)[1] - 1 + 127, 0) - down, 1)
    scale = np.exp2(byte - 127.0)
    codes = (blocks / scale).astype(np.float32).astype(dtype).astype(np.float64)
    return np.moveaxis((codes * scale).reshape(v.shape), -1, axis)


WIDE = False


def mx_kscale(k):
    if not WIDE:
        return np.ones(k)
    levels = np.array([10, -10, 5, -5, 0])
    if k % 512:
        return np.exp2(np.random.permutation(np.resize(levels, k // 32))).repeat(32)
    a = np.empty((k // 512, 16))
    for p in range(k // 512):
        a[p, :8] = np.random.permutation(np.resize(levels, 8))
        for g in range(8):
            far = levels[np.abs(levels - a[p, g]) >= 10]
            a[p, g + 8] = far[np.random.randint(len(far))]
    return np.exp2(a.ravel()).repeat(32)


def f64(x):
    return np.asarray(x).astype(np.float64)


def striped(idx):
    return np.tile(idx.reshape(-1, 16).T, (8, 1)).astype(np.uint16)


def unstriped(offs):
    return offs[:16].T.reshape(-1).astype(np.int64)


E2M1 = np.array([0.0, 0.5, 1.0, 1.5, 2.0, 3.0, 4.0, 6.0, -0.0, -0.5, -1.0, -1.5, -2.0, -3.0, -4.0, -6.0])


def pack_weight(w, fmt):
    k, n = w.shape
    w = f64(np.asarray(w, np.float32).astype(ml_dtypes.bfloat16)).reshape(k // 32, 32, n)
    amax = np.abs(w).max(1)
    if fmt == "e4m3":
        byte = np.frexp(amax)[1] - 1 + 127 - 7
    else:
        mant, ex = np.frexp(amax / 6.0)
        byte = np.where(mant > 0.5, ex, ex - 1) + 127
    byte = np.clip(np.where(amax > 0, byte, 1), 1, 254)
    scaled = (w * np.exp2(127.0 - byte)[:, None, :]).reshape(k, n).astype(np.float32)
    by_word = np.ascontiguousarray(scaled.reshape(k // 512, 128, 4, n).transpose(0, 1, 3, 2))
    if fmt == "e4m3":
        words = by_word.astype(ml_dtypes.float8_e4m3fn).view(np.uint8)
    else:
        c = by_word.astype(ml_dtypes.float4_e2m1fn).view(np.uint8) & 0xF
        words = (c[..., 0::2] | (c[..., 1::2] << 4)).reshape(k // 512, 128, 2 * n)
    return np.ascontiguousarray(words), np.ascontiguousarray(byte.astype(np.uint8).reshape(k // 512, 16, n))


def unpack_weight(words, scales, fmt):
    g, _, n = scales.shape
    words = np.ascontiguousarray(words).reshape(g, 128, n, -1)
    if fmt == "e4m3":
        vals = words.view(ml_dtypes.float8_e4m3fn).astype(np.float64)
    else:
        nib = np.empty((g, 128, n, 4), np.uint8)
        nib[..., 0::2] = words & 0xF
        nib[..., 1::2] = words >> 4
        vals = E2M1[nib]
    vals = vals * np.repeat(np.exp2(scales.astype(np.float64) - 127.0), 8, axis=1)[..., None]
    return vals.transpose(0, 1, 3, 2).reshape(g * 512, n)


def gelu(v):
    return 0.5 * v * (1.0 + np.tanh(np.sqrt(2.0 / np.pi) * (v + 0.044715 * v**3)))


def often(T, S):
    return np.random.permutation(T)[(T * np.random.uniform(0, 1, S) ** 4).astype(np.int64)]


T, S, P, K, K2, H, N = 4096, 1024, 512, 1024, 512, 1024, 512


def setup_inputs():
    n = np.random.standard_normal
    s = mx_kscale(K)[:, None]
    s2 = mx_kscale(K2)[:, None]
    u = mx_kscale(H)[:, None]
    d = {}
    d["tab_words"], d["tab_scales"] = pack_weight(n((K, T)) * s, "e4m3")
    d["tab2_words"], d["tab2_scales"] = pack_weight(n((K2, T)) * s2, "e4m3")
    d["tab3_words"], d["tab3_scales"] = pack_weight(n((K2, T)) * s2, "e4m3")
    d["offs"] = striped(np.random.permutation(T)[:S])
    d["offs2"] = striped(np.random.permutation(T)[:S])
    d["offs3"] = striped(np.random.permutation(T)[:S])
    d["pos1"] = striped(np.random.permutation(S)[:P])
    d["pos2"] = striped(often(S, P))
    d["pos3"] = striped(often(S, P))
    d["w1"] = (n((K, H)) / K ** 0.5 / s * u.T).astype(np.float32)
    d["w2_words"], d["w2_scales"] = pack_weight(1.3 * n((K2, H)) / K2 ** 0.5 / s2 * u.T, "e2m1")
    d["w3"] = (1.2 * n((K2, H)) / K2 ** 0.5 / s2).astype(np.float32)
    d["w4_words"], d["w4_scales"] = pack_weight(n((H, N)) / H ** 0.5 / u, "e4m3")
    d["soak"] = np.exp(0.4 * n((H, S))).astype(np.float32)
    d["swing"] = np.random.uniform(1.4, 2.8, H).astype(np.float32)
    d["least"] = (0.6 * n(N)).astype(np.float32)
    return d


def reference(tab_words, tab_scales, tab2_words, tab2_scales, tab3_words, tab3_scales, offs, offs2, offs3,
              pos1, pos2, pos3, w1, w2_words, w2_scales, w3, w4_words, w4_scales, soak, swing, least):
    v = unpack_weight(tab_words, tab_scales, "e4m3")[:, unstriped(offs)]
    v2 = unpack_weight(tab2_words, tab2_scales, "e4m3")[:, unstriped(offs2)]
    v3 = unpack_weight(tab3_words, tab3_scales, "e4m3")[:, unstriped(offs3)]
    a = f64(soak) * (mxq(f64(w1), 0, "e4m3").T @ v)
    b = unpack_weight(w2_words, w2_scales, "e2m1").T @ v2
    d = f64(swing)[:, None] * np.tanh(mxq(f64(w3), 0, "e4m3").T @ v3)
    z = a[:, unstriped(pos1)] - b[:, unstriped(pos2)] * np.cos(d[:, unstriped(pos3)])
    y = unpack_weight(w4_words, w4_scales, "e4m3").T @ mxq(z, 0, "e4m3")
    return np.maximum(y, f64(least)[:, None])

import math
from contextlib import ExitStack

import concourse.mybir as mybir

T, S, PICK, K, K2, H, N = 4096, 1024, 512, 1024, 512, 1024, 512
FLOPS = 2 * S * H * (K + 2 * K2) + 2 * H * N * PICK

F32 = mybir.dt.float32
BF16 = mybir.dt.bfloat16
I32 = mybir.dt.int32
U32 = mybir.dt.uint32
U16 = mybir.dt.uint16
U8 = mybir.dt.uint8
FP8X4 = mybir.dt.float8_e4m3fn_x4
FP4X4 = mybir.dt.float4_e2m1fn_x4
ALU = mybir.AluOpType
ACT = mybir.ActivationFunctionType

P = 128
PACK = 4
PASS = P * PACK
BANK = 512
QUADS = 4
HALF = PICK // 2


def tile_list_hide_drum_finish_kernel(
    tc, tab_words, tab_scales, tab2_words, tab2_scales, tab3_words, tab3_scales, offs, offs2, offs3,
    pos1, pos2, pos3, w1, w2_words, w2_scales, w3, w4_words, w4_scales, soak, swing, least, out,
):
    nc = tc.nc
    blocks = H // PASS
    row_tiles = [(b, t) for b in range(blocks) for t in range(PACK)]

    with ExitStack() as ctx:
        lists = ctx.enter_context(tc.tile_pool(name="lists", bufs=1))
        keep = ctx.enter_context(tc.tile_pool(name="keep", bufs=1))
        work = ctx.enter_context(tc.tile_pool(name="work", bufs=1))
        psum = ctx.enter_context(tc.psum_pool(name="psum", bufs=1))

        def load_list(src, name):
            tile = lists.tile([P, src.shape[1]], U16, name=name)
            nc.sync.dma_start(tile[:], src)
            return tile

        def window_tile(dtype, columns):
            return work.tile([P, columns], dtype, name="window", tag="window", bufs=8, align_bytes=64)

        def load_table_scales(scales, queue):
            passes = scales.shape[0]
            tile = window_tile(U8, T)
            nc.vector.memset(tile[:].bitcast(I32), 0)
            for q in range(QUADS):
                queue.dma_start(
                    tile[32 * q : 32 * q + 4 * passes, :].bitcast(I32),
                    scales[:, 4 * q : 4 * q + 4, :].bitcast(I32),
                )
            return tile

        def load_table_words(words, a):
            tile = work.tile([P, T], U32, name="big", tag="big", bufs=4, align_bytes=64)
            nc.sync.dma_start(tile[:].bitcast(I32), words[a].rearrange("p n i -> p (n i)").bitcast(I32))
            return tile

        def gather(window, offsets, dtype, name):
            tile = keep.tile([P, S], dtype, name=name, align_bytes=64)
            nc.vector.tensor_copy(tile[:], window[:].indirect(offsets[:]))
            return tile

        def load_weight(w, a, b):
            tile = work.tile([P, PACK, PASS], F32, name="wide", tag="wide", bufs=4, align_bytes=64)
            rows = w[PASS * a : PASS * (a + 1), PASS * b : PASS * (b + 1)]
            nc.sync.dma_start(tile[:], rows.rearrange("(p i) c -> p i c", i=PACK))
            return tile

        def round_weight(raw):
            tile = work.tile([P, PASS * PACK], BF16, name="rounded", tag="rounded", bufs=2, align_bytes=64)
            nc.scalar.copy(
                tile[:].rearrange("p (t m i) -> p m t i", t=PACK, i=PACK),
                raw[:].rearrange("p i (m t) -> p m t i", t=PACK),
            )
            return tile

        def quantize(rounded, columns, name):
            codes = keep.tile([P, columns], U32, name=name + "_codes", align_bytes=64)
            scales = keep.tile([P, columns], U8, name=name + "_scales", align_bytes=64)
            nc.vector.quantize_mx(out=codes[:].bitcast(FP8X4), scales=scales[:], in_=rounded)
            return codes, scales

        def first_stage(passes, h):
            bank = psum.tile([P, BANK], F32, name="acc", tag="acc", bufs=4)
            cols = slice(BANK * h, BANK * (h + 1))
            for n, (lhs, lhs_scale, rhs, rhs_scale) in enumerate(passes):
                nc.tensor.matmul_mx(
                    out=bank[:], lhsT=lhs, lhsT_scale=lhs_scale, rhs=rhs[:, cols].bitcast(FP8X4),
                    rhs_scale=rhs_scale[:, cols], start=(n == 0), stop=(n == len(passes) - 1),
                )
            return bank, cols

        tab3_s = load_table_scales(tab3_scales, nc.sync)
        offs3_t = load_list(offs3, "offs3")
        tab3_w = load_table_words(tab3_words, 0)
        w3_raw = [load_weight(w3, 0, 0)]
        tab2_s = load_table_scales(tab2_scales, nc.sync)
        offs2_t = load_list(offs2, "offs2")
        w3_raw.append(load_weight(w3, 0, 1))
        pos3_t = load_list(pos3, "pos3")
        tab_s = load_table_scales(tab_scales, nc.sync)
        offs_t = load_list(offs, "offs")
        tab2_w = load_table_words(tab2_words, 0)
        w2_raw = keep.tile([P, 2 * H], U8, name="w2_raw", align_bytes=64)
        nc.sync.dma_start(w2_raw[:].bitcast(I32), w2_words[0].bitcast(I32))
        w2_raw_s = keep.tile([P, H], U8, name="w2_raw_s", align_bytes=64)
        nc.vector.memset(w2_raw_s[:].bitcast(I32), 0)
        for q in range(QUADS):
            nc.sync.dma_start(
                w2_raw_s[32 * q : 32 * q + 4, :].bitcast(I32), w2_scales[0, 4 * q : 4 * q + 4, :].bitcast(I32)
            )
        swing_t = keep.tile([P, blocks, PACK], F32, name="swing")
        nc.sync.dma_start(swing_t[:], swing.rearrange("(b p t) -> p b t", b=blocks, t=PACK))
        pos2_t = load_list(pos2, "pos2")
        pos1_t = load_list(pos1, "pos1")
        w1_raw = {(a, 0): load_weight(w1, a, 0) for a in range(K // PASS)}
        tab_w = [load_table_words(tab_words, a) for a in range(K // PASS)]

        def load_soak(b):
            tile = work.tile([P, PACK, S], F32, name="big", tag="big", bufs=4, align_bytes=64)
            rows = soak[PASS * b : PASS * (b + 1), :].rearrange("(p t) j -> p t j", t=PACK)
            for t in range(PACK):
                nc.sync.dma_start(tile[:, t, :], rows[:, t, :])
            return tile


        v3_s = gather(tab3_s, offs3_t, U8, "v3_s")
        v3 = gather(tab3_w, offs3_t, U32, "v3")
        v2_s = gather(tab2_s, offs2_t, U8, "v2_s")

        w2_c = keep.tile([P, 2 * H], U8, name="w2_c", align_bytes=64)
        nc.gpsimd.tensor_copy(
            w2_c[:].rearrange("p (b t m e) -> p b t m e", b=blocks, t=PACK, e=2),
            w2_raw[:].rearrange("p (b m t e) -> p b t m e", b=blocks, t=PACK, e=2),
        )
        w2_s = keep.tile([P, H], U8, name="w2_s", align_bytes=64)
        nc.gpsimd.tensor_copy(
            w2_s[:].rearrange("p (b t m) -> p b t m", b=blocks, t=PACK),
            w2_raw_s[:].rearrange("p (b m t) -> p b t m", b=blocks, t=PACK),
        )

        w3_q = [quantize(round_weight(w3_raw[b])[:], PASS, "w3_%d" % b) for b in range(blocks)]
        v_s = gather(tab_s, offs_t, U8, "v_s")
        v2 = gather(tab2_w, offs2_t, U32, "v2")
        soak_t = [load_soak(0)]

        tanh_w = {}
        for b, t in row_tiles:
            m = slice(P * t, P * (t + 1))
            tanh_w[b, t] = window_tile(F32, S)
            for h in range(S // BANK):
                bank, cols = first_stage([(w3_q[b][0][:, m].bitcast(FP8X4), w3_q[b][1][:, m], v3, v3_s)], h)
                nc.scalar.activation(tanh_w[b, t][:, cols], bank[:], ACT.Tanh)

        half_pi = keep.tile([P, 1], F32, name="half_pi", tag="w3_1_scales", align_bytes=64)
        one = keep.tile([P, 1], F32, name="one")
        nc.vector.memset(one[:], 1.0)
        nc.vector.tensor_scalar(half_pi[:], one[:], math.pi / 2, None, ALU.mult)

        for a in range(K // PASS):
            w1_raw[a, 1] = load_weight(w1, a, 1)
        w4_c = keep.tile([P, blocks, N], U32, name="w4_c", align_bytes=64)
        nc.sync.dma_start(w4_c[:].bitcast(I32), w4_words.rearrange("a p n i -> p a (n i)").bitcast(I32))
        w4_s = keep.tile([P, blocks, N], U8, name="w4_s", align_bytes=64)
        nc.vector.memset(w4_s[:].bitcast(I32), 0)
        for q in range(QUADS):
            nc.sync.dma_start(
                w4_s[32 * q : 32 * q + 4, :, :].bitcast(I32),
                w4_scales[:, 4 * q : 4 * q + 4, :].rearrange("a r n -> r a n").bitcast(I32),
            )
        least_t = keep.tile([P, N // P], F32, name="least")
        with nc.allow_non_contiguous_dma(reason="one value of least for each partition and output tile"):
            nc.sync.dma_start(least_t[:], least.rearrange("(i p) -> p i", p=P))
        soak_t.append(load_soak(1))

        def small(name, bufs):
            return work.tile([P, PICK], F32, name=name, tag=name, bufs=bufs, align_bytes=64)

        turned = {}
        w1_q = {}
        for n, (b, t) in enumerate(row_tiles):
            picked = small("picked", 3)
            nc.vector.tensor_copy(picked[:], tanh_w[b, t][:].indirect(pos3_t[:]))
            size = small("size", 2)
            nc.scalar.activation(size[:], picked[:], ACT.Abs, scale=swing_t[:, b, t : t + 1])
            cos = small("cos", 3)
            nc.scalar.activation(cos[:], size[:], ACT.Sin, bias=half_pi[:], scale=-1.0)
            drum = window_tile(F32, S)
            c0 = PASS * b + P * t
            for h in range(S // BANK):
                lhs = w2_c[:, 2 * c0 : 2 * (c0 + P)].bitcast(FP4X4)
                bank, cols = first_stage([(lhs, w2_s[:, c0 : c0 + P], v2, v2_s)], h)
                nc.scalar.copy(drum[:, cols], bank[:])
            turned[b, t] = small("turned", 8)
            nc.vector.tensor_tensor(turned[b, t][:], drum[:].indirect(pos2_t[:]), cos[:], ALU.mult)
            if t == PACK - 1:
                for a in range(K // PASS):
                    w1_q[a, b] = quantize(round_weight(w1_raw[a, b])[:], PASS, "w1_%d%d" % (a, b))
            if n == 1:
                v = [gather(tab_w[a], offs_t, U32, "v_%d" % a) for a in range(K // PASS)]

        y = [[psum.tile([P, BANK], F32, name="y%d%d" % (h, q)) for q in range(2)] for h in range(2)]
        for b in range(blocks):
            z = work.tile([P, PACK, PICK], F32, name="wide", tag="wide", bufs=4, align_bytes=64)
            for t in range(PACK):
                m = slice(P * t, P * (t + 1))
                hide = window_tile(F32, S)
                for h in range(S // BANK):
                    passes = [
                        (w1_q[a, b][0][:, m].bitcast(FP8X4), w1_q[a, b][1][:, m], v[a], v_s[4 * a :, :])
                        for a in range(K // PASS)
                    ]
                    bank, cols = first_stage(passes, h)
                    nc.vector.tensor_tensor(hide[:, cols], bank[:], soak_t[b][:, t, cols], ALU.mult)
                nc.vector.tensor_tensor(z[:, t, :], hide[:].indirect(pos1_t[:]), turned[b, t][:], ALU.subtract)
            for h in range(2):
                j = slice(HALF * h, HALF * (h + 1))
                rounded = work.tile([P, HALF * PACK], BF16, name="z_rounded", tag="z_rounded", bufs=2, align_bytes=64)
                dst = rounded[:].rearrange("p (c i t) -> p c t i", i=4, t=PACK)
                src = z[:, :, j].rearrange("p t (c i) -> p c t i", i=4)
                if b == blocks - 1 and h == 1:
                    nc.vector.tensor_copy(dst, src)
                else:
                    nc.scalar.copy(dst, src)
                z_c, z_s = quantize(rounded[:], HALF, "z_%d%d" % (b, h))
                for i in range(N // P):
                    nc.tensor.matmul_mx(
                        out=y[h][i // 2][:, HALF * (i % 2) : HALF * (i % 2 + 1)],
                        lhsT=w4_c[:, b, P * i : P * (i + 1)].bitcast(FP8X4),
                        lhsT_scale=w4_s[:, b, P * i : P * (i + 1)],
                        rhs=z_c[:].bitcast(FP8X4), rhs_scale=z_s[:],
                        start=(b == 0 and i % 2 == 0), stop=(b == blocks - 1 and i % 2 == 1),
                    )

        for h in range(2):
            result = keep.tile([P, N // P, HALF], F32, name="result%d" % h)
            for i in range(N // P):
                nc.vector.tensor_scalar(
                    result[:, i, :], y[h][i // 2][:, HALF * (i % 2) : HALF * (i % 2 + 1)],
                    least_t[:, i : i + 1], None, ALU.max,
                )
            nc.sync.dma_start(out[:, HALF * h : HALF * (h + 1)].rearrange("(i p) j -> p i j", p=P), result[:])
